import numpy as np
import ml_dtypes


def mxq(x, axis, fmt="e4m3"):
    dtype, down = {"e4m3": (ml_dtypes.float8_e4m3fn, 7), "e5m2": (ml_dtypes.float8_e5m2, 14)}[fmt]
    v = np.moveaxis(np.asarray(x, np.float32).astype(ml_dtypes.bfloat16).astype(np.float64), axis, -1)
    blocks = v.reshape(v.shape[:-1] + (-1, 32))
    amax = np.abs(blocks).max(-1, keepdims=True)
    byte = np.maximum(np.where(amax > 0, np.frexp(amax)[1] - 1 + 127, 0) - down, 1)
    scale = np.exp2(byte - 127.0)
    codes = (blocks / scale).astype(np.float32).astype(dtype).astype(np.float64)
    return np.moveaxis((codes * scale).reshape(v.shape), -1, axis)


WIDE = False


def mx_kscale(k):
    if not WIDE:
        return np.ones(k)
    levels = np.array([10, -10, 5, -5, 0])
    if k % 512:
        return np.exp2(np.random.permutation(np.resize(levels, k // 32))).repeat(32)
    a = np.empty((k // 512, 16))
    for p in range(k // 512):
        a[p, :8] = np.random.permutation(np.resize(levels, 8))
        for g in range(8):
            far = levels[np.abs(levels - a[p, g]) >= 10]
            a[p, g + 8] = far[np.random.randint(len(far))]
    return np.exp2(a.ravel()).repeat(32)


def f64(x):
    return np.asarray(x).astype(np.float64)


def striped(idx):
    return np.tile(idx.reshape(-1, 16).T, (8, 1)).astype(np.uint16)


def unstriped(offs):
    return offs[:16].T.reshape(-1).astype(np.int64)


def pack_weight(w):
    k, n = w.shape
    w = f64(np.asarray(w, np.float32).astype(ml_dtypes.bfloat16)).reshape(k // 32, 32, n)
    amax = np.abs(w).max(1)
    byte = np.clip(np.where(amax > 0, np.frexp(amax)[1] - 1 + 127 - 7, 1), 1, 254)
    scaled = (w * np.exp2(127.0 - byte)[:, None, :]).reshape(k, n).astype(np.float32)
    words = np.ascontiguousarray(scaled.reshape(k // 512, 128, 4, n).transpose(0, 1, 3, 2)).astype(ml_dtypes.float8_e4m3fn).view(np.uint8)
    return words, np.ascontiguousarray(byte.astype(np.uint8).reshape(k // 512, 16, n))


def unpack_weight(words, scales):
    g, p, n, _ = words.shape
    vals = np.ascontiguousarray(words).view(ml_dtypes.float8_e4m3fn).astype(np.float64) * np.repeat(np.exp2(scales.astype(np.float64) - 127.0), 8, axis=1)[..., None]
    return vals.transpose(0, 1, 3, 2).reshape(g * 512, n)


E2M1 = np.array([0.0, 0.5, 1.0, 1.5, 2.0, 3.0, 4.0, 6.0, -0.0, -0.5, -1.0, -1.5, -2.0, -3.0, -4.0, -6.0])


def pack_fp4(w):
    k, n = w.shape
    w = f64(np.asarray(w, np.float32).astype(ml_dtypes.bfloat16)).reshape(k // 32, 32, n)
    amax = np.abs(w).max(1)
    mant, ex = np.frexp(amax / 6.0)
    byte = np.clip(np.where(amax > 0, np.where(mant > 0.5, ex, ex - 1) + 127, 1), 1, 254)
    scaled = (w * np.exp2(127.0 - byte)[:, None, :]).reshape(k, n).astype(np.float32)
    c = np.ascontiguousarray(scaled.reshape(k // 512, 128, 4, n).transpose(0, 1, 3, 2)).astype(ml_dtypes.float4_e2m1fn).view(np.uint8) & 0xF
    words = (c[..., 0::2] | (c[..., 1::2] << 4)).reshape(k // 512, 128, 2 * n)
    return np.ascontiguousarray(words), np.ascontiguousarray(byte.astype(np.uint8).reshape(k // 512, 16, n))


def unpack_fp4(words, scales):
    g, _, n = scales.shape
    words = np.ascontiguousarray(words).reshape(g, 128, n, 2)
    nib = np.empty((g, 128, n, 4), np.uint8)
    nib[..., 0::2] = words & 0xF
    nib[..., 1::2] = words >> 4
    vals = E2M1[nib] * np.repeat(np.exp2(scales.astype(np.float64) - 127.0), 8, axis=1)[..., None]
    return vals.transpose(0, 1, 3, 2).reshape(g * 512, n)


def sigmoid(v):
    return 1.0 / (1.0 + np.exp(-np.maximum(v, -700.0)))


K, T, S, N, H = 512, 2048, 512, 256, 512


def setup_inputs():
    n = np.random.standard_normal
    s = mx_kscale(K)[:, None]
    u = mx_kscale(H)
    packed_xT = pack_weight(n((K, T)) * s)
    packed_w1 = pack_fp4(n((K, H)) / np.sqrt(K) / s)
    packed_w2 = pack_fp4(n((H, N)) / np.sqrt(H) / u[:, None])
    return {
        "x_words": packed_xT[0],
        "x_scales": packed_xT[1],
        "w1_words": packed_w1[0],
        "w1_scales": packed_w1[1],
        "unit": (np.random.uniform(0.6, 1.4, (H, 1)) * u[:, None]).astype(np.float32),
        "w2_words": packed_w2[0],
        "w2_scales": packed_w2[1],
        "offs": striped(np.random.permutation(T)[:S]),
        "g2": striped(np.random.permutation(S)),
        "g3": striped(np.random.permutation(S)),
    }


def reference(x_words, x_scales, w1_words, w1_scales, unit, w2_words, w2_scales, offs, g2, g3):
    xq = unpack_weight(x_words, x_scales)[:, unstriped(offs)]
    y = unpack_fp4(w1_words, w1_scales).T @ xq
    adj = (sigmoid(y)) ** 2
    ag = adj[:, unstriped(g2)]
    ah = adj[:, unstriped(g3)]
    shared = adj * ag + ah * adj[:, unstriped(g2)]
    conn = adj.mean(axis=1, keepdims=True)
    tom = (shared + adj) / (np.minimum(adj, adj[:, unstriped(g2)]) + conn + 0.6)
    dtom = -1.0 * tom + 1.0
    hid = f64(unit) * (dtom * y)
    return unpack_fp4(w2_words, w2_scales).T @ mxq(hid, 0, "e4m3")

@@ -1,0 +1,270 @@
+from contextlib import ExitStack
+
+import concourse.mybir as mybir
+
+K, T, S, N, H = 512, 2048, 512, 256, 512
+FLOPS = 2 * K * H * S + 2 * H * N * S
+
+F32 = mybir.dt.float32
+BF16 = mybir.dt.bfloat16
+I32 = mybir.dt.int32
+U32 = mybir.dt.uint32
+U16 = mybir.dt.uint16
+U8 = mybir.dt.uint8
+FP8X4 = mybir.dt.float8_e4m3fn_x4
+FP4X4 = mybir.dt.float4_e2m1fn_x4
+ALU = mybir.AluOpType
+ACT = mybir.ActivationFunctionType
+
+P = 128
+PACK = 4
+HALF = S // 2
+LIST_HALF = HALF // 16
+
+
+def tile_picked_ytopov_dis_p_kernel(
+    tc, x_words, x_scales, w1_words, w1_scales, unit, w2_words, w2_scales, offs, g2, g3, out
+):
+    nc = tc.nc
+    with ExitStack() as ctx:
+        keep = ctx.enter_context(tc.tile_pool(name="keep", bufs=1))
+        psum = ctx.enter_context(tc.psum_pool(name="psum", bufs=1))
+
+        def sb(name, shape, dtype):
+            return keep.tile(shape, dtype, name=name, align_bytes=64)
+
+        offs_t = sb("offs_t", [P, S // 16], U16)
+        g2_t = sb("g2_t", [P, S // 16], U16)
+        g3_t = sb("g3_t", [P, S // 16], U16)
+        xw = sb("xw", [P, T], I32)
+        xs = sb("xs", [P, T], U8)
+        w1w = sb("w1w", [P, 2 * H], U8)
+        w1s = sb("w1s", [P, H], U8)
+        w2w = sb("w2w", [P, 2 * N], U8)
+        w2s = sb("w2s", [P, N], U8)
+        u = sb("u", [P, PACK], F32)
+
+        nc.vector.memset(w1s[:].bitcast(I32), 0)
+        nc.vector.memset(xs[:, : T // 2].bitcast(I32), 0)
+        nc.gpsimd.memset(xs[:, T // 2 :].bitcast(I32), 0)
+        nc.gpsimd.memset(w2s[:].bitcast(I32), 0)
+
+        def load_scale_rows(queue, tile, dram, q):
+            queue.dma_start(
+                out=tile[32 * q : 32 * q + 4, :].bitcast(I32),
+                in_=dram[0, 4 * q : 4 * q + 4, :].bitcast(I32),
+            )
+
+        nc.sync.dma_start(offs_t[:], offs)
+        nc.scalar.dma_start(out=w1w[:].bitcast(I32), in_=w1_words[0].bitcast(I32))
+        nc.sync.dma_start(out=xw[:], in_=x_words[0].rearrange("p n t -> p (n t)").bitcast(I32))
+        load_scale_rows(nc.scalar, w1s, w1_scales, 0)
+        load_scale_rows(nc.gpsimd, w1s, w1_scales, 2)
+        load_scale_rows(nc.gpsimd, w1s, w1_scales, 3)
+        load_scale_rows(nc.sync, xs, x_scales, 0)
+        load_scale_rows(nc.scalar, xs, x_scales, 1)
+        load_scale_rows(nc.sync, xs, x_scales, 2)
+        load_scale_rows(nc.scalar, xs, x_scales, 3)
+        load_scale_rows(nc.sync, w1s, w1_scales, 1)
+        nc.sync.dma_start(g2_t[:], g2)
+        nc.sync.dma_start(g3_t[:], g3)
+        nc.sync.dma_start(out=u[:], in_=unit.rearrange("(p t) o -> p (t o)", t=PACK))
+        nc.sync.dma_start(out=w2w[:].bitcast(I32), in_=w2_words[0].bitcast(I32))
+        for q in range(4):
+            load_scale_rows(nc.sync, w2s, w2_scales, q)
+
+        def cols(h):
+            return slice(h * HALF, (h + 1) * HALF)
+
+        def entries(h):
+            return slice(h * LIST_HALF, (h + 1) * LIST_HALF)
+
+        whole = slice(0, S)
+        xq_s = sb("xq_s", [P, S], U8)
+        xq_w = sb("xq_w", [P, S], U32)
+        w1w_d = sb("w1w_d", [P, PACK, 2 * P], U8)
+        w1s_d = sb("w1s_d", [P, PACK, P], U8)
+        nc.vector.tensor_copy(
+            out=w1w_d[:].rearrange("p t (m b) -> p t m b", b=2),
+            in_=w1w[:].rearrange("p (m t b) -> p t m b", t=PACK, b=2),
+        )
+        nc.vector.tensor_copy(xq_s[:], xs[:].indirect(offs_t[:]))
+        nc.vector.tensor_copy(out=w1s_d[:], in_=w1s[:].rearrange("p (m t) -> p t m", t=PACK))
+        for h in range(2):
+            nc.vector.tensor_copy(xq_w[:, cols(h)], xw[:].bitcast(U32).indirect(offs_t[:, entries(h)]))
+
+        y0 = [psum.tile([P, HALF], F32, name="y0_%d" % h) for h in range(2)]
+        y = [None] + [psum.tile([P, S], F32, name="y%d" % t) for t in range(1, PACK)]
+
+        def y_half(t, h):
+            return y0[h][:] if t == 0 else y[t][:, cols(h)]
+
+        def project(dst, t, c):
+            nc.tensor.matmul_mx(
+                out=dst,
+                lhsT=w1w_d[:, t, :].bitcast(FP4X4),
+                lhsT_scale=w1s_d[:, t, :],
+                rhs=xq_w[:, c].bitcast(FP8X4),
+                rhs_scale=xq_s[:, c],
+                start=True,
+                stop=True,
+            )
+
+        for h in range(2):
+            project(y0[h][:], 0, cols(h))
+        for t in range(1, PACK):
+            project(y[t][:], t, whole)
+
+        neg_u = sb("neg_u", [P, PACK], F32)
+
+        sig = [sb("sig%d" % t, [P, S], F32) for t in range(PACK)]
+        adj = [sb("adj%d" % t, [P, S], F32) for t in range(PACK)]
+        ag = [sb("ag%d" % t, [P, S], F32) for t in range(PACK)]
+        ah = sb("ah", [P, S], F32)
+        low = [sb("low%d" % t, [P, S], F32) for t in range(PACK)]
+        den2 = [sb("den2_%d" % t, [P, S], F32) for t in range(PACK)]
+        rden = [sb("rden%d" % t, [P, S], F32) for t in range(PACK)]
+        ahag = [sb("ahag%d" % t, [P, S], F32) for t in range(PACK)]
+        own = [sb("own%d" % t, [P, S], F32) for t in range(PACK)]
+        num = [sb("num%d" % t, [P, S], F32) for t in range(PACK)]
+        utom = [sb("utom%d" % t, [P, S], F32) for t in range(PACK)]
+        row_sum = [sb("row_sum%d" % t, [P, 2], F32) for t in range(PACK)]
+        base = [sb("base%d" % t, [P, 1], F32) for t in range(PACK)]
+        hid = [sb("hid%d" % h, [P, PACK, HALF], BF16) for h in range(2)]
+        woven = [sb("woven%d" % h, [P, HALF * PACK], BF16) for h in range(2)]
+
+        def sigmoid(t):
+            nc.scalar.activation(sig[t][:], y[t][:], ACT.Sigmoid)
+
+        def square_on_vector(t, c, k):
+            nc.vector.scalar_tensor_tensor(
+                adj[t][:, c], sig[t][:, c], 1.0, sig[t][:, c], ALU.mult, ALU.mult, accum_out=row_sum[t][:, k : k + 1]
+            )
+
+        def square_on_scalar(t):
+            nc.scalar.activation(adj[t][:], sig[t][:], ACT.Square, accum_out=row_sum[t][:, 0:1])
+
+        def mean(t):
+            if t == 0:
+                nc.vector.tensor_scalar(base[t][:], row_sum[t][:, 0:1], row_sum[t][:, 1:2], 0.6 * S, ALU.add, ALU.add)
+            else:
+                nc.vector.tensor_scalar(base[t][:], row_sum[t][:, 0:1], 0.6 * S, None, ALU.add)
+
+        def fetch(dst, t, lst, h):
+            nc.scalar.activation(dst[:, cols(h)], adj[t][:].indirect(lst[:, entries(h)]), ACT.Copy)
+
+        def fetch_ag(t):
+            for h in range(2):
+                fetch(ag[t], t, g2_t, h)
+
+        def smaller(t, c):
+            nc.vector.tensor_tensor(low[t][:, c], adj[t][:, c], ag[t][:, c], ALU.min)
+
+        def far_product(t, h):
+            if t == PACK - 1:
+                nc.vector.tensor_tensor(ahag[t][:, cols(h)], ah[:, cols(h)], ag[t][:, cols(h)], ALU.mult)
+            else:
+                nc.vector.tensor_tensor(
+                    ahag[t][:, cols(h)], adj[t][:].indirect(g3_t[:, entries(h)]), ag[t][:, cols(h)], ALU.mult
+                )
+
+        def own_product(t, c):
+            nc.vector.scalar_tensor_tensor(own[t][:, c], ag[t][:, c], 1.0, adj[t][:, c], ALU.add, ALU.mult)
+
+        def numerator(t, c):
+            nc.vector.tensor_tensor(num[t][:, c], ahag[t][:, c], own[t][:, c], ALU.add)
+
+        def reciprocal(t, c):
+            nc.scalar.activation(den2[t][:, c], low[t][:, c], ACT.Square, bias=base[t][:], scale=float(S))
+            nc.scalar.activation(rden[t][:, c], den2[t][:, c], ACT.Abs_reciprocal_sqrt)
+
+        def ratio(t, c):
+            nc.vector.scalar_tensor_tensor(
+                utom[t][:, c], num[t][:, c], neg_u[:, t : t + 1], rden[t][:, c], ALU.mult, ALU.mult
+            )
+
+        def hidden(t, h):
+            nc.vector.scalar_tensor_tensor(
+                hid[h][:, t, :], utom[t][:, cols(h)], u[:, t : t + 1], y_half(t, h), ALU.add, ALU.mult
+            )
+
+        def weave(h, engine_copy):
+            engine_copy(
+                woven[h][:].rearrange("p (c i t) -> p c t i", i=4, t=PACK),
+                hid[h][:].rearrange("p t (c i) -> p c t i", i=4),
+            )
+
+        def finish(h):
+            codes = sb("codes%d" % h, [P, HALF], U32)
+            scales = sb("scales%d" % h, [P, HALF], U8)
+            nc.vector.quantize_mx(out=codes[:].bitcast(FP8X4), scales=scales[:], in_=woven[h][:])
+            acc = psum.tile([P, 2, HALF], F32, name="acc%d" % h)
+            for mh in range(2):
+                nc.tensor.matmul_mx(
+                    out=acc[:, mh, :],
+                    lhsT=w2w[:, 2 * P * mh : 2 * P * (mh + 1)].bitcast(FP4X4),
+                    lhsT_scale=w2s[:, P * mh : P * (mh + 1)],
+                    rhs=codes[:].bitcast(FP8X4),
+                    rhs_scale=scales[:],
+                    start=True,
+                    stop=True,
+                )
+            res = sb("res%d" % h, [P, 2, HALF], F32)
+            nc.scalar.copy(res[:], acc[:])
+            nc.sync.dma_start(out=out.rearrange("(mh p) j -> p mh j", p=P)[:, :, cols(h)], in_=res[:])
+
+        for h in range(2):
+            nc.scalar.activation(sig[0][:, cols(h)], y0[h][:], ACT.Sigmoid)
+            square_on_vector(0, cols(h), h)
+        sigmoid(1)
+        fetch_ag(0)
+        square_on_vector(1, whole, 0)
+        sigmoid(2)
+        sigmoid(3)
+        for h in range(2):
+            smaller(0, cols(h))
+            far_product(0, h)
+            own_product(0, cols(h))
+        mean(0)
+        mean(1)
+        nc.vector.tensor_scalar(neg_u[:], u[:], -float(S), None, ALU.mult)
+        fetch_ag(1)
+        numerator(0, whole)
+        square_on_scalar(2)
+        fetch_ag(2)
+        for t in (1, 2):
+            smaller(t, whole)
+            far_product(t, 0)
+            far_product(t, 1)
+            own_product(t, whole)
+            if t == 1:
+                mean(2)
+                reciprocal(0, whole)
+                reciprocal(1, whole)
+            numerator(t, whole)
+        square_on_scalar(3)
+        fetch_ag(3)
+        ratio(0, whole)
+        ratio(1, whole)
+        mean(3)
+        reciprocal(2, whole)
+        for t in range(2):
+            for h in range(2):
+                hidden(t, h)
+        smaller(3, whole)
+        for h in range(2):
+            fetch(ah, 3, g3_t, h)
+            reciprocal(3, cols(h))
+        for h in range(2):
+            own_product(3, cols(h))
+            ratio(2, cols(h))
+            far_product(3, h)
+            hidden(2, h)
+            numerator(3, cols(h))
+            ratio(3, cols(h))
+            hidden(3, h)
+            if h == 0:
+                weave(0, nc.scalar.copy)
+        finish(0)
+        weave(1, nc.vector.tensor_copy)
+        finish(1)

@@ -1,3 +1,4 @@
+import math
 from contextlib import ExitStack
 
 import concourse.mybir as mybir
@@ -19,7 +20,9 @@ ACT = mybir.ActivationFunctionType
 P = 128
 PACK = 4
 HALF = S // 2
-LIST_HALF = HALF // 16
+EARLY_COLUMNS = 704
+PARTS = (slice(0, 256), slice(256, 512))
+VECTOR_WEAVE = 176
 
 
 def tile_picked_ytopov_dis_p_kernel(
@@ -44,10 +47,10 @@ def tile_picked_ytopov_dis_p_kernel(
         w2s = sb("w2s", [P, N], U8)
         u = sb("u", [P, PACK], F32)
 
-        nc.vector.memset(w1s[:].bitcast(I32), 0)
         nc.vector.memset(xs[:, : T // 2].bitcast(I32), 0)
         nc.gpsimd.memset(xs[:, T // 2 :].bitcast(I32), 0)
-        nc.gpsimd.memset(w2s[:].bitcast(I32), 0)
+        nc.vector.memset(w1s[:].bitcast(I32), 0)
+        nc.vector.memset(w2s[:].bitcast(I32), 0)
 
         def load_scale_rows(queue, tile, dram, q):
             queue.dma_start(
@@ -55,17 +58,15 @@ def tile_picked_ytopov_dis_p_kernel(
                 in_=dram[0, 4 * q : 4 * q + 4, :].bitcast(I32),
             )
 
+        x_rows = x_words[0].rearrange("p n t -> p (n t)").bitcast(I32)
         nc.sync.dma_start(offs_t[:], offs)
         nc.scalar.dma_start(out=w1w[:].bitcast(I32), in_=w1_words[0].bitcast(I32))
-        nc.sync.dma_start(out=xw[:], in_=x_words[0].rearrange("p n t -> p (n t)").bitcast(I32))
-        load_scale_rows(nc.scalar, w1s, w1_scales, 0)
-        load_scale_rows(nc.gpsimd, w1s, w1_scales, 2)
-        load_scale_rows(nc.gpsimd, w1s, w1_scales, 3)
-        load_scale_rows(nc.sync, xs, x_scales, 0)
-        load_scale_rows(nc.scalar, xs, x_scales, 1)
-        load_scale_rows(nc.sync, xs, x_scales, 2)
-        load_scale_rows(nc.scalar, xs, x_scales, 3)
-        load_scale_rows(nc.sync, w1s, w1_scales, 1)
+        nc.scalar.dma_start(out=xw[:, :EARLY_COLUMNS], in_=x_rows[:, :EARLY_COLUMNS])
+        for q in range(4):
+            load_scale_rows(nc.sync if q % 2 == 0 else nc.scalar, xs, x_scales, q)
+        nc.sync.dma_start(out=xw[:, EARLY_COLUMNS:], in_=x_rows[:, EARLY_COLUMNS:])
+        for q in range(4):
+            load_scale_rows(nc.scalar, w1s, w1_scales, q)
         nc.sync.dma_start(g2_t[:], g2)
         nc.sync.dma_start(g3_t[:], g3)
         nc.sync.dma_start(out=u[:], in_=unit.rearrange("(p t) o -> p (t o)", t=PACK))
@@ -73,13 +74,12 @@ def tile_picked_ytopov_dis_p_kernel(
         for q in range(4):
             load_scale_rows(nc.sync, w2s, w2_scales, q)
 
-        def cols(h):
-            return slice(h * HALF, (h + 1) * HALF)
-
-        def entries(h):
-            return slice(h * LIST_HALF, (h + 1) * LIST_HALF)
-
         whole = slice(0, S)
+        halves = (slice(0, HALF), slice(HALF, S))
+
+        def entries(c):
+            return slice(c.start // 16, c.stop // 16)
+
         xq_s = sb("xq_s", [P, S], U8)
         xq_w = sb("xq_w", [P, S], U32)
         w1w_d = sb("w1w_d", [P, PACK, 2 * P], U8)
@@ -89,15 +89,13 @@ def tile_picked_ytopov_dis_p_kernel(
             in_=w1w[:].rearrange("p (m t b) -> p t m b", t=PACK, b=2),
         )
         nc.vector.tensor_copy(xq_s[:], xs[:].indirect(offs_t[:]))
-        nc.vector.tensor_copy(out=w1s_d[:], in_=w1s[:].rearrange("p (m t) -> p t m", t=PACK))
-        for h in range(2):
-            nc.vector.tensor_copy(xq_w[:, cols(h)], xw[:].bitcast(U32).indirect(offs_t[:, entries(h)]))
+        nc.vector.tensor_copy(xq_w[:], xw[:].bitcast(U32).indirect(offs_t[:]))
+        w1s_by_tile = w1s[:].rearrange("p (m t) -> p t m", t=PACK)
+        nc.vector.tensor_copy(out=w1s_d[:, 0, :], in_=w1s_by_tile[:, 0, :])
+        nc.vector.tensor_copy(out=w1s_d[:, 1:, :], in_=w1s_by_tile[:, 1:, :])
 
         y0 = [psum.tile([P, HALF], F32, name="y0_%d" % h) for h in range(2)]
         y = [None] + [psum.tile([P, S], F32, name="y%d" % t) for t in range(1, PACK)]
-
-        def y_half(t, h):
-            return y0[h][:] if t == 0 else y[t][:, cols(h)]
 
         def project(dst, t, c):
             nc.tensor.matmul_mx(
@@ -111,14 +109,15 @@ def tile_picked_ytopov_dis_p_kernel(
             )
 
         for h in range(2):
-            project(y0[h][:], 0, cols(h))
+            project(y0[h][:], 0, halves[h])
         for t in range(1, PACK):
             project(y[t][:], t, whole)
 
         neg_u = sb("neg_u", [P, PACK], F32)
-
-        sig = [sb("sig%d" % t, [P, S], F32) for t in range(PACK)]
-        adj = [sb("adj%d" % t, [P, S], F32) for t in range(PACK)]
+        sig = sb("sig", [P, PACK, S + 16], F32)
+        adj = [sb("adj%d" % t, [P, S + 1], F32) for t in range(PACK)]
+        half_sums = sb("half_sums", [P, 2], F32)
+        base = sb("base", [P, PACK], F32)
         ag = [sb("ag%d" % t, [P, S], F32) for t in range(PACK)]
         ah = sb("ah", [P, S], F32)
         low = [sb("low%d" % t, [P, S], F32) for t in range(PACK)]
@@ -128,54 +127,39 @@ def tile_picked_ytopov_dis_p_kernel(
         own = [sb("own%d" % t, [P, S], F32) for t in range(PACK)]
         num = [sb("num%d" % t, [P, S], F32) for t in range(PACK)]
         utom = [sb("utom%d" % t, [P, S], F32) for t in range(PACK)]
-        row_sum = [sb("row_sum%d" % t, [P, 2], F32) for t in range(PACK)]
-        base = [sb("base%d" % t, [P, 1], F32) for t in range(PACK)]
-        hid = [sb("hid%d" % h, [P, PACK, HALF], BF16) for h in range(2)]
-        woven = [sb("woven%d" % h, [P, HALF * PACK], BF16) for h in range(2)]
+
+        ones = sb("ones", [P, PACK], F32)
+        nc.vector.memset(ones[:], 1.0)
+        nc.vector.tensor_scalar(sig[:, :, S], ones[:], math.sqrt(0.6 * S), None, ALU.mult)
 
         def sigmoid(t):
-            nc.scalar.activation(sig[t][:], y[t][:], ACT.Sigmoid)
+            nc.scalar.activation(sig[:, t, whole], y[t][:], ACT.Sigmoid)
 
-        def square_on_vector(t, c, k):
-            nc.vector.scalar_tensor_tensor(
-                adj[t][:, c], sig[t][:, c], 1.0, sig[t][:, c], ALU.mult, ALU.mult, accum_out=row_sum[t][:, k : k + 1]
-            )
+        def square(t):
+            nc.scalar.activation(adj[t][:], sig[:, t, : S + 1], ACT.Square, accum_out=base[:, t : t + 1])
 
-        def square_on_scalar(t):
-            nc.scalar.activation(adj[t][:], sig[t][:], ACT.Square, accum_out=row_sum[t][:, 0:1])
+        def fetch(dst, t, lst, c):
+            nc.scalar.activation(dst[:, c], adj[t][:].indirect(lst[:, entries(c)]), ACT.Copy)
 
-        def mean(t):
-            if t == 0:
-                nc.vector.tensor_scalar(base[t][:], row_sum[t][:, 0:1], row_sum[t][:, 1:2], 0.6 * S, ALU.add, ALU.add)
+        def smaller(t):
+            nc.vector.tensor_tensor(low[t][:], adj[t][:, whole], ag[t][:], ALU.min)
+
+        def far_product(t, c):
+            if t == 3:
+                nc.vector.tensor_tensor(ahag[t][:, c], ah[:, c], ag[t][:, c], ALU.mult)
             else:
-                nc.vector.tensor_scalar(base[t][:], row_sum[t][:, 0:1], 0.6 * S, None, ALU.add)
+                nc.vector.tensor_tensor(ahag[t][:, c], adj[t][:].indirect(g3_t[:, entries(c)]), ag[t][:, c], ALU.mult)
 
-        def fetch(dst, t, lst, h):
-            nc.scalar.activation(dst[:, cols(h)], adj[t][:].indirect(lst[:, entries(h)]), ACT.Copy)
+        def own_product(t):
+            nc.vector.scalar_tensor_tensor(own[t][:], ag[t][:], 1.0, adj[t][:, whole], ALU.add, ALU.mult)
 
-        def fetch_ag(t):
-            for h in range(2):
-                fetch(ag[t], t, g2_t, h)
+        def numerator(t):
+            nc.vector.tensor_tensor(num[t][:], ahag[t][:], own[t][:], ALU.add)
 
-        def smaller(t, c):
-            nc.vector.tensor_tensor(low[t][:, c], adj[t][:, c], ag[t][:, c], ALU.min)
-
-        def far_product(t, h):
-            if t == PACK - 1:
-                nc.vector.tensor_tensor(ahag[t][:, cols(h)], ah[:, cols(h)], ag[t][:, cols(h)], ALU.mult)
-            else:
-                nc.vector.tensor_tensor(
-                    ahag[t][:, cols(h)], adj[t][:].indirect(g3_t[:, entries(h)]), ag[t][:, cols(h)], ALU.mult
-                )
-
-        def own_product(t, c):
-            nc.vector.scalar_tensor_tensor(own[t][:, c], ag[t][:, c], 1.0, adj[t][:, c], ALU.add, ALU.mult)
-
-        def numerator(t, c):
-            nc.vector.tensor_tensor(num[t][:, c], ahag[t][:, c], own[t][:, c], ALU.add)
+        def denominator(t, c):
+            nc.scalar.activation(den2[t][:, c], low[t][:, c], ACT.Square, bias=base[:, t : t + 1], scale=float(S))
 
         def reciprocal(t, c):
-            nc.scalar.activation(den2[t][:, c], low[t][:, c], ACT.Square, bias=base[t][:], scale=float(S))
             nc.scalar.activation(rden[t][:, c], den2[t][:, c], ACT.Abs_reciprocal_sqrt)
 
         def ratio(t, c):
@@ -183,25 +167,34 @@ def tile_picked_ytopov_dis_p_kernel(
                 utom[t][:, c], num[t][:, c], neg_u[:, t : t + 1], rden[t][:, c], ALU.mult, ALU.mult
             )
 
-        def hidden(t, h):
-            nc.vector.scalar_tensor_tensor(
-                hid[h][:, t, :], utom[t][:, cols(h)], u[:, t : t + 1], y_half(t, h), ALU.add, ALU.mult
-            )
+        def hidden(dst, t, c):
+            h = c.start // HALF
+            y_run = y0[h][:, c.start - h * HALF : c.stop - h * HALF] if t == 0 else y[t][:, c]
+            nc.vector.scalar_tensor_tensor(dst[:, t, :], utom[t][:, c], u[:, t : t + 1], y_run, ALU.add, ALU.mult)
 
-        def weave(h, engine_copy):
+        def weave(woven, hid, lo, hi, engine_copy):
             engine_copy(
-                woven[h][:].rearrange("p (c i t) -> p c t i", i=4, t=PACK),
-                hid[h][:].rearrange("p t (c i) -> p c t i", i=4),
+                woven[:, PACK * lo : PACK * hi].rearrange("p (c i t) -> p c t i", i=4, t=PACK),
+                hid[:, :, lo:hi].rearrange("p t (c i) -> p c t i", i=4),
             )
 
-        def finish(h):
-            codes = sb("codes%d" % h, [P, HALF], U32)
-            scales = sb("scales%d" % h, [P, HALF], U8)
-            nc.vector.quantize_mx(out=codes[:].bitcast(FP8X4), scales=scales[:], in_=woven[h][:])
-            acc = psum.tile([P, 2, HALF], F32, name="acc%d" % h)
+        out_v = out.rearrange("(mh p) j -> p mh j", p=P)
+
+        def finish(k, woven):
+            c = PARTS[k]
+            n = c.stop - c.start
+            codes = sb("codes%d" % k, [P, n], U32)
+            scales = sb("scales%d" % k, [P, n], U8)
+            nc.vector.quantize_mx(out=codes[:].bitcast(FP8X4), scales=scales[:], in_=woven[:])
+            last = k == len(PARTS) - 1
+            if last:
+                acc = [psum.tile([P, n], F32, name="acc_last%d" % mh)[:] for mh in range(2)]
+            else:
+                both = psum.tile([P, 2, n], F32, name="acc%d" % k)
+                acc = [both[:, mh, :] for mh in range(2)]
             for mh in range(2):
                 nc.tensor.matmul_mx(
-                    out=acc[:, mh, :],
+                    out=acc[mh],
                     lhsT=w2w[:, 2 * P * mh : 2 * P * (mh + 1)].bitcast(FP4X4),
                     lhsT_scale=w2s[:, P * mh : P * (mh + 1)],
                     rhs=codes[:].bitcast(FP8X4),
@@ -209,62 +202,66 @@ def tile_picked_ytopov_dis_p_kernel(
                     start=True,
                     stop=True,
                 )
-            res = sb("res%d" % h, [P, 2, HALF], F32)
-            nc.scalar.copy(res[:], acc[:])
-            nc.sync.dma_start(out=out.rearrange("(mh p) j -> p mh j", p=P)[:, :, cols(h)], in_=res[:])
+            if last:
+                for mh, (copy_out, queue) in enumerate(((nc.scalar.copy, nc.scalar), (nc.vector.tensor_copy, nc.sync))):
+                    res = sb("res_last%d" % mh, [P, n], F32)
+                    copy_out(res[:], acc[mh])
+                    queue.dma_start(out=out_v[:, mh, c], in_=res[:])
+            else:
+                res = sb("res%d" % k, [P, 2, n], F32)
+                nc.scalar.copy(res[:], both[:])
+                nc.sync.dma_start(out=out_v[:, :, c], in_=res[:])
 
-        for h in range(2):
-            nc.scalar.activation(sig[0][:, cols(h)], y0[h][:], ACT.Sigmoid)
-            square_on_vector(0, cols(h), h)
+        for h, c in enumerate((halves[0], slice(HALF, S + 1))):
+            nc.scalar.activation(sig[:, 0, halves[h]], y0[h][:], ACT.Sigmoid)
+            nc.vector.scalar_tensor_tensor(
+                adj[0][:, c], sig[:, 0, c], 1.0, sig[:, 0, c], ALU.mult, ALU.mult, accum_out=half_sums[:, h : h + 1]
+            )
+        nc.vector.tensor_copy(ag[0][:, halves[0]], adj[0][:].indirect(g2_t[:, entries(halves[0])]))
         sigmoid(1)
-        fetch_ag(0)
-        square_on_vector(1, whole, 0)
+        fetch(ag[0], 0, g2_t, halves[1])
+        square(1)
+        fetch(ag[1], 1, g2_t, whole)
+        far_product(0, halves[0])
+        far_product(0, halves[1])
+        smaller(0)
+        own_product(0)
         sigmoid(2)
         sigmoid(3)
-        for h in range(2):
-            smaller(0, cols(h))
-            far_product(0, h)
-            own_product(0, cols(h))
-        mean(0)
-        mean(1)
+        for t in (2, 3):
+            square(t)
+            fetch(ag[t], t, g2_t, whole)
+        fetch(ah, 3, g3_t, whole)
+        nc.vector.tensor_tensor(base[:, 0:1], half_sums[:, 0:1], half_sums[:, 1:2], ALU.add)
         nc.vector.tensor_scalar(neg_u[:], u[:], -float(S), None, ALU.mult)
-        fetch_ag(1)
-        numerator(0, whole)
-        square_on_scalar(2)
-        fetch_ag(2)
-        for t in (1, 2):
-            smaller(t, whole)
-            far_product(t, 0)
-            far_product(t, 1)
-            own_product(t, whole)
-            if t == 1:
-                mean(2)
-                reciprocal(0, whole)
-                reciprocal(1, whole)
-            numerator(t, whole)
-        square_on_scalar(3)
-        fetch_ag(3)
-        ratio(0, whole)
-        ratio(1, whole)
-        mean(3)
-        reciprocal(2, whole)
-        for t in range(2):
-            for h in range(2):
-                hidden(t, h)
-        smaller(3, whole)
-        for h in range(2):
-            fetch(ah, 3, g3_t, h)
-            reciprocal(3, cols(h))
-        for h in range(2):
-            own_product(3, cols(h))
-            ratio(2, cols(h))
-            far_product(3, h)
-            hidden(2, h)
-            numerator(3, cols(h))
-            ratio(3, cols(h))
-            hidden(3, h)
-            if h == 0:
-                weave(0, nc.scalar.copy)
-        finish(0)
-        weave(1, nc.vector.tensor_copy)
-        finish(1)
+        for t in range(1, PACK):
+            smaller(t)
+            numerator(t - 1)
+            own_product(t)
+            far_product(t, whole)
+        for k, c in enumerate(PARTS):
+            for t in range(PACK):
+                if k == 0:
+                    denominator(t, whole)
+                reciprocal(t, c)
+        pending = None
+        for k, c in enumerate(PARTS):
+            n = c.stop - c.start
+            hid = sb("hid%d" % k, [P, PACK, n], BF16)
+            woven = sb("woven%d" % k, [P, PACK * n], BF16)
+            for t in range(PACK):
+                ratio(t, c)
+                if k == 0 and t == 0:
+                    numerator(PACK - 1)
+                if t > 0:
+                    hidden(hid, t - 1, c)
+                if t == 3 and pending is not None:
+                    finish(*pending)
+            hidden(hid, PACK - 1, c)
+            if k < len(PARTS) - 1:
+                weave(woven, hid, 0, n, nc.scalar.copy)
+                pending = (k, woven)
+            else:
+                weave(woven, hid, 0, VECTOR_WEAVE, nc.vector.tensor_copy)
+                weave(woven, hid, VECTOR_WEAVE, n, nc.scalar.copy)
+                finish(k, woven)

@@ -141,8 +141,8 @@ def tile_picked_ytopov_dis_p_kernel(
         def fetch(dst, t, lst, c):
             nc.scalar.activation(dst[:, c], adj[t][:].indirect(lst[:, entries(c)]), ACT.Copy)
 
-        def smaller(t):
-            nc.vector.tensor_tensor(low[t][:], adj[t][:, whole], ag[t][:], ALU.min)
+        def smaller(t, c=whole):
+            nc.vector.tensor_tensor(low[t][:, c], adj[t][:, c], ag[t][:, c], ALU.min)
 
         def far_product(t, c):
             if t == 3:
@@ -150,8 +150,8 @@ def tile_picked_ytopov_dis_p_kernel(
             else:
                 nc.vector.tensor_tensor(ahag[t][:, c], adj[t][:].indirect(g3_t[:, entries(c)]), ag[t][:, c], ALU.mult)
 
-        def own_product(t):
-            nc.vector.scalar_tensor_tensor(own[t][:], ag[t][:], 1.0, adj[t][:, whole], ALU.add, ALU.mult)
+        def own_product(t, c=whole):
+            nc.vector.scalar_tensor_tensor(own[t][:, c], ag[t][:, c], 1.0, adj[t][:, c], ALU.add, ALU.mult)
 
         def numerator(t):
             nc.vector.tensor_tensor(num[t][:], ahag[t][:], own[t][:], ALU.add)
@@ -219,13 +219,13 @@ def tile_picked_ytopov_dis_p_kernel(
             )
         nc.vector.tensor_copy(ag[0][:, halves[0]], adj[0][:].indirect(g2_t[:, entries(halves[0])]))
         sigmoid(1)
-        fetch(ag[0], 0, g2_t, halves[1])
         square(1)
+        fetch(ag[0], 0, g2_t, halves[1])
         fetch(ag[1], 1, g2_t, whole)
-        far_product(0, halves[0])
-        far_product(0, halves[1])
-        smaller(0)
-        own_product(0)
+        for c in halves:
+            far_product(0, c)
+            smaller(0, c)
+            own_product(0, c)
         sigmoid(2)
         sigmoid(3)
         for t in (2, 3):
@@ -241,8 +241,7 @@ def tile_picked_ytopov_dis_p_kernel(
             far_product(t, whole)
         for k, c in enumerate(PARTS):
             for t in range(PACK):
-                if k == 0:
-                    denominator(t, whole)
+                denominator(t, c)
                 reciprocal(t, c)
         pending = None
         for k, c in enumerate(PARTS):

import math
from contextlib import ExitStack

import concourse.mybir as mybir

K, T, S, N, H = 512, 2048, 512, 256, 512
FLOPS = 2 * K * H * S + 2 * H * N * S

F32 = mybir.dt.float32
BF16 = mybir.dt.bfloat16
I32 = mybir.dt.int32
U32 = mybir.dt.uint32
U16 = mybir.dt.uint16
U8 = mybir.dt.uint8
FP8X4 = mybir.dt.float8_e4m3fn_x4
FP4X4 = mybir.dt.float4_e2m1fn_x4
ALU = mybir.AluOpType
ACT = mybir.ActivationFunctionType

P = 128
PACK = 4
HALF = S // 2
EARLY_COLUMNS = 704
PARTS = (slice(0, 256), slice(256, 512))
VECTOR_WEAVE = 176


def tile_picked_ytopov_dis_p_kernel(
    tc, x_words, x_scales, w1_words, w1_scales, unit, w2_words, w2_scales, offs, g2, g3, out
):
    nc = tc.nc
    with ExitStack() as ctx:
        keep = ctx.enter_context(tc.tile_pool(name="keep", bufs=1))
        psum = ctx.enter_context(tc.psum_pool(name="psum", bufs=1))

        def sb(name, shape, dtype):
            return keep.tile(shape, dtype, name=name, align_bytes=64)

        offs_t = sb("offs_t", [P, S // 16], U16)
        g2_t = sb("g2_t", [P, S // 16], U16)
        g3_t = sb("g3_t", [P, S // 16], U16)
        xw = sb("xw", [P, T], I32)
        xs = sb("xs", [P, T], U8)
        w1w = sb("w1w", [P, 2 * H], U8)
        w1s = sb("w1s", [P, H], U8)
        w2w = sb("w2w", [P, 2 * N], U8)
        w2s = sb("w2s", [P, N], U8)
        u = sb("u", [P, PACK], F32)

        nc.vector.memset(xs[:, : T // 2].bitcast(I32), 0)
        nc.gpsimd.memset(xs[:, T // 2 :].bitcast(I32), 0)
        nc.vector.memset(w1s[:].bitcast(I32), 0)
        nc.vector.memset(w2s[:].bitcast(I32), 0)

        def load_scale_rows(queue, tile, dram, q):
            queue.dma_start(
                out=tile[32 * q : 32 * q + 4, :].bitcast(I32),
                in_=dram[0, 4 * q : 4 * q + 4, :].bitcast(I32),
            )

        x_rows = x_words[0].rearrange("p n t -> p (n t)").bitcast(I32)
        nc.sync.dma_start(offs_t[:], offs)
        nc.scalar.dma_start(out=w1w[:].bitcast(I32), in_=w1_words[0].bitcast(I32))
        nc.scalar.dma_start(out=xw[:, :EARLY_COLUMNS], in_=x_rows[:, :EARLY_COLUMNS])
        for q in range(4):
            load_scale_rows(nc.sync if q % 2 == 0 else nc.scalar, xs, x_scales, q)
        nc.sync.dma_start(out=xw[:, EARLY_COLUMNS:], in_=x_rows[:, EARLY_COLUMNS:])
        for q in range(4):
            load_scale_rows(nc.scalar, w1s, w1_scales, q)
        nc.sync.dma_start(g2_t[:], g2)
        nc.sync.dma_start(g3_t[:], g3)
        nc.sync.dma_start(out=u[:], in_=unit.rearrange("(p t) o -> p (t o)", t=PACK))
        nc.sync.dma_start(out=w2w[:].bitcast(I32), in_=w2_words[0].bitcast(I32))
        for q in range(4):
            load_scale_rows(nc.sync, w2s, w2_scales, q)

        whole = slice(0, S)
        halves = (slice(0, HALF), slice(HALF, S))

        def entries(c):
            return slice(c.start // 16, c.stop // 16)

        xq_s = sb("xq_s", [P, S], U8)
        xq_w = sb("xq_w", [P, S], U32)
        w1w_d = sb("w1w_d", [P, PACK, 2 * P], U8)
        w1s_d = sb("w1s_d", [P, PACK, P], U8)
        nc.vector.tensor_copy(
            out=w1w_d[:].rearrange("p t (m b) -> p t m b", b=2),
            in_=w1w[:].rearrange("p (m t b) -> p t m b", t=PACK, b=2),
        )
        nc.vector.tensor_copy(xq_s[:], xs[:].indirect(offs_t[:]))
        nc.vector.tensor_copy(xq_w[:], xw[:].bitcast(U32).indirect(offs_t[:]))
        w1s_by_tile = w1s[:].rearrange("p (m t) -> p t m", t=PACK)
        nc.vector.tensor_copy(out=w1s_d[:, 0, :], in_=w1s_by_tile[:, 0, :])
        nc.vector.tensor_copy(out=w1s_d[:, 1:, :], in_=w1s_by_tile[:, 1:, :])

        y0 = [psum.tile([P, HALF], F32, name="y0_%d" % h) for h in range(2)]
        y = [None] + [psum.tile([P, S], F32, name="y%d" % t) for t in range(1, PACK)]

        def project(dst, t, c):
            nc.tensor.matmul_mx(
                out=dst,
                lhsT=w1w_d[:, t, :].bitcast(FP4X4),
                lhsT_scale=w1s_d[:, t, :],
                rhs=xq_w[:, c].bitcast(FP8X4),
                rhs_scale=xq_s[:, c],
                start=True,
                stop=True,
            )

        for h in range(2):
            project(y0[h][:], 0, halves[h])
        for t in range(1, PACK):
            project(y[t][:], t, whole)

        neg_u = sb("neg_u", [P, PACK], F32)
        sig = sb("sig", [P, PACK, S + 16], F32)
        adj = [sb("adj%d" % t, [P, S + 1], F32) for t in range(PACK)]
        half_sums = sb("half_sums", [P, 2], F32)
        base = sb("base", [P, PACK], F32)
        ag = [sb("ag%d" % t, [P, S], F32) for t in range(PACK)]
        ah = sb("ah", [P, S], F32)
        low = [sb("low%d" % t, [P, S], F32) for t in range(PACK)]
        den2 = [sb("den2_%d" % t, [P, S], F32) for t in range(PACK)]
        rden = [sb("rden%d" % t, [P, S], F32) for t in range(PACK)]
        ahag = [sb("ahag%d" % t, [P, S], F32) for t in range(PACK)]
        own = [sb("own%d" % t, [P, S], F32) for t in range(PACK)]
        num = [sb("num%d" % t, [P, S], F32) for t in range(PACK)]
        utom = [sb("utom%d" % t, [P, S], F32) for t in range(PACK)]

        ones = sb("ones", [P, PACK], F32)
        nc.vector.memset(ones[:], 1.0)
        nc.vector.tensor_scalar(sig[:, :, S], ones[:], math.sqrt(0.6 * S), None, ALU.mult)

        def sigmoid(t):
            nc.scalar.activation(sig[:, t, whole], y[t][:], ACT.Sigmoid)

        def square(t):
            nc.scalar.activation(adj[t][:], sig[:, t, : S + 1], ACT.Square, accum_out=base[:, t : t + 1])

        def fetch(dst, t, lst, c):
            nc.scalar.activation(dst[:, c], adj[t][:].indirect(lst[:, entries(c)]), ACT.Copy)

        def smaller(t, c=whole):
            nc.vector.tensor_tensor(low[t][:, c], adj[t][:, c], ag[t][:, c], ALU.min)

        def far_product(t, c):
            if t == 3:
                nc.vector.tensor_tensor(ahag[t][:, c], ah[:, c], ag[t][:, c], ALU.mult)
            else:
                nc.vector.tensor_tensor(ahag[t][:, c], adj[t][:].indirect(g3_t[:, entries(c)]), ag[t][:, c], ALU.mult)

        def own_product(t, c=whole):
            nc.vector.scalar_tensor_tensor(own[t][:, c], ag[t][:, c], 1.0, adj[t][:, c], ALU.add, ALU.mult)

        def numerator(t):
            nc.vector.tensor_tensor(num[t][:], ahag[t][:], own[t][:], ALU.add)

        def denominator(t, c):
            nc.scalar.activation(den2[t][:, c], low[t][:, c], ACT.Square, bias=base[:, t : t + 1], scale=float(S))

        def reciprocal(t, c):
            nc.scalar.activation(rden[t][:, c], den2[t][:, c], ACT.Abs_reciprocal_sqrt)

        def ratio(t, c):
            nc.vector.scalar_tensor_tensor(
                utom[t][:, c], num[t][:, c], neg_u[:, t : t + 1], rden[t][:, c], ALU.mult, ALU.mult
            )

        def hidden(dst, t, c):
            h = c.start // HALF
            y_run = y0[h][:, c.start - h * HALF : c.stop - h * HALF] if t == 0 else y[t][:, c]
            nc.vector.scalar_tensor_tensor(dst[:, t, :], utom[t][:, c], u[:, t : t + 1], y_run, ALU.add, ALU.mult)

        def weave(woven, hid, lo, hi, engine_copy):
            engine_copy(
                woven[:, PACK * lo : PACK * hi].rearrange("p (c i t) -> p c t i", i=4, t=PACK),
                hid[:, :, lo:hi].rearrange("p t (c i) -> p c t i", i=4),
            )

        out_v = out.rearrange("(mh p) j -> p mh j", p=P)

        def finish(k, woven):
            c = PARTS[k]
            n = c.stop - c.start
            codes = sb("codes%d" % k, [P, n], U32)
            scales = sb("scales%d" % k, [P, n], U8)
            nc.vector.quantize_mx(out=codes[:].bitcast(FP8X4), scales=scales[:], in_=woven[:])
            last = k == len(PARTS) - 1
            if last:
                acc = [psum.tile([P, n], F32, name="acc_last%d" % mh)[:] for mh in range(2)]
            else:
                both = psum.tile([P, 2, n], F32, name="acc%d" % k)
                acc = [both[:, mh, :] for mh in range(2)]
            for mh in range(2):
                nc.tensor.matmul_mx(
                    out=acc[mh],
                    lhsT=w2w[:, 2 * P * mh : 2 * P * (mh + 1)].bitcast(FP4X4),
                    lhsT_scale=w2s[:, P * mh : P * (mh + 1)],
                    rhs=codes[:].bitcast(FP8X4),
                    rhs_scale=scales[:],
                    start=True,
                    stop=True,
                )
            if last:
                for mh, (copy_out, queue) in enumerate(((nc.scalar.copy, nc.scalar), (nc.vector.tensor_copy, nc.sync))):
                    res = sb("res_last%d" % mh, [P, n], F32)
                    copy_out(res[:], acc[mh])
                    queue.dma_start(out=out_v[:, mh, c], in_=res[:])
            else:
                res = sb("res%d" % k, [P, 2, n], F32)
                nc.scalar.copy(res[:], both[:])
                nc.sync.dma_start(out=out_v[:, :, c], in_=res[:])

        for h, c in enumerate((halves[0], slice(HALF, S + 1))):
            nc.scalar.activation(sig[:, 0, halves[h]], y0[h][:], ACT.Sigmoid)
            nc.vector.scalar_tensor_tensor(
                adj[0][:, c], sig[:, 0, c], 1.0, sig[:, 0, c], ALU.mult, ALU.mult, accum_out=half_sums[:, h : h + 1]
            )
        nc.vector.tensor_copy(ag[0][:, halves[0]], adj[0][:].indirect(g2_t[:, entries(halves[0])]))
        sigmoid(1)
        square(1)
        fetch(ag[0], 0, g2_t, halves[1])
        fetch(ag[1], 1, g2_t, whole)
        for c in halves:
            far_product(0, c)
            smaller(0, c)
            own_product(0, c)
        sigmoid(2)
        sigmoid(3)
        for t in (2, 3):
            square(t)
            fetch(ag[t], t, g2_t, whole)
        fetch(ah, 3, g3_t, whole)
        nc.vector.tensor_tensor(base[:, 0:1], half_sums[:, 0:1], half_sums[:, 1:2], ALU.add)
        nc.vector.tensor_scalar(neg_u[:], u[:], -float(S), None, ALU.mult)
        for t in range(1, PACK):
            smaller(t)
            numerator(t - 1)
            own_product(t)
            far_product(t, whole)
        for k, c in enumerate(PARTS):
            for t in range(PACK):
                denominator(t, c)
                reciprocal(t, c)
        pending = None
        for k, c in enumerate(PARTS):
            n = c.stop - c.start
            hid = sb("hid%d" % k, [P, PACK, n], BF16)
            woven = sb("woven%d" % k, [P, PACK * n], BF16)
            for t in range(PACK):
                ratio(t, c)
                if k == 0 and t == 0:
                    numerator(PACK - 1)
                if t > 0:
                    hidden(hid, t - 1, c)
                if t == 3 and pending is not None:
                    finish(*pending)
            hidden(hid, PACK - 1, c)
            if k < len(PARTS) - 1:
                weave(woven, hid, 0, n, nc.scalar.copy)
                pending = (k, woven)
            else:
                weave(woven, hid, 0, VECTOR_WEAVE, nc.vector.tensor_copy)
                weave(woven, hid, VECTOR_WEAVE, n, nc.scalar.copy)
                finish(k, woven)
